import numpy as np
import ml_dtypes


def mxq(x, axis, fmt="e4m3"):
    dtype, down = {"e4m3": (ml_dtypes.float8_e4m3fn, 7), "e5m2": (ml_dtypes.float8_e5m2, 14)}[fmt]
    v = np.moveaxis(np.asarray(x, np.float32).astype(ml_dtypes.bfloat16).astype(np.float64), axis, -1)
    blocks = v.reshape(v.shape[:-1] + (-1, 32))
    amax = np.abs(blocks).max(-1, keepdims=True)
    byte = np.maximum(np.where(amax > 0, np.frexp(amax)[1] - 1 + 127, 0) - down, 1)
    scale = np.exp2(byte - 127.0)
    codes = (blocks / scale).astype(np.float32).astype(dtype).astype(np.float64)
    return np.moveaxis((codes * scale).reshape(v.shape), -1, axis)


WIDE = False


def mx_kscale(k):
    if not WIDE:
        return np.ones(k)
    levels = np.array([10, -10, 5, -5, 0])
    if k % 512:
        return np.exp2(np.random.permutation(np.resize(levels, k // 32))).repeat(32)
    a = np.empty((k // 512, 16))
    for p in range(k // 512):
        a[p, :8] = np.random.permutation(np.resize(levels, 8))
        for g in range(8):
            far = levels[np.abs(levels - a[p, g]) >= 10]
            a[p, g + 8] = far[np.random.randint(len(far))]
    return np.exp2(a.ravel()).repeat(32)


def f64(x):
    return np.asarray(x).astype(np.float64)


def striped(idx):
    return np.tile(idx.reshape(-1, 16).T, (8, 1)).astype(np.uint16)


def unstriped(offs):
    return offs[:16].T.reshape(-1).astype(np.int64)


def striped8(idx):
    return np.concatenate([x.reshape(-1, 16).T for x in idx]).astype(np.uint16)


def runs(offs, k):
    lists = np.stack([offs[16 * r : 16 * r + 16].T.reshape(-1) for r in range(8)]).astype(np.int64)
    return lists[np.arange(k) % 512 // 64]


def pack_weight(w):
    k, n = w.shape
    w = f64(np.asarray(w, np.float32).astype(ml_dtypes.bfloat16)).reshape(k // 32, 32, n)
    amax = np.abs(w).max(1)
    byte = np.clip(np.where(amax > 0, np.frexp(amax)[1] - 1 + 127 - 7, 1), 1, 254)
    scaled = (w * np.exp2(127.0 - byte)[:, None, :]).reshape(k, n).astype(np.float32)
    words = np.ascontiguousarray(scaled.reshape(k // 512, 128, 4, n).transpose(0, 1, 3, 2)).astype(ml_dtypes.float8_e4m3fn).view(np.uint8)
    return words, np.ascontiguousarray(byte.astype(np.uint8).reshape(k // 512, 16, n))


def unpack_weight(words, scales):
    g, p, n, _ = words.shape
    vals = np.ascontiguousarray(words).view(ml_dtypes.float8_e4m3fn).astype(np.float64) * np.repeat(np.exp2(scales.astype(np.float64) - 127.0), 8, axis=1)[..., None]
    return vals.transpose(0, 1, 3, 2).reshape(g * 512, n)


E2M1 = np.array([0.0, 0.5, 1.0, 1.5, 2.0, 3.0, 4.0, 6.0, -0.0, -0.5, -1.0, -1.5, -2.0, -3.0, -4.0, -6.0])


def pack_fp4(w):
    k, n = w.shape
    w = f64(np.asarray(w, np.float32).astype(ml_dtypes.bfloat16)).reshape(k // 32, 32, n)
    amax = np.abs(w).max(1)
    mant, ex = np.frexp(amax / 6.0)
    byte = np.clip(np.where(amax > 0, np.where(mant > 0.5, ex, ex - 1) + 127, 1), 1, 254)
    scaled = (w * np.exp2(127.0 - byte)[:, None, :]).reshape(k, n).astype(np.float32)
    c = np.ascontiguousarray(scaled.reshape(k // 512, 128, 4, n).transpose(0, 1, 3, 2)).astype(ml_dtypes.float4_e2m1fn).view(np.uint8) & 0xF
    words = (c[..., 0::2] | (c[..., 1::2] << 4)).reshape(k // 512, 128, 2 * n)
    return np.ascontiguousarray(words), np.ascontiguousarray(byte.astype(np.uint8).reshape(k // 512, 16, n))


def unpack_fp4(words, scales):
    g, _, n = scales.shape
    words = np.ascontiguousarray(words).reshape(g, 128, n, 2)
    nib = np.empty((g, 128, n, 4), np.uint8)
    nib[..., 0::2] = words & 0xF
    nib[..., 1::2] = words >> 4
    vals = E2M1[nib] * np.repeat(np.exp2(scales.astype(np.float64) - 127.0), 8, axis=1)[..., None]
    return vals.transpose(0, 1, 3, 2).reshape(g * 512, n)


def relu(v):
    return np.maximum(v, 0.0)

def planes(y):
    n, m = y.shape
    v = y.astype(np.float32).astype(ml_dtypes.bfloat16).astype(np.float64).reshape(n // 32, 32, m)
    top = np.abs(v).max(1)
    byte = np.clip(np.where(top > 0, np.frexp(top)[1] - 1 + 127 - 7, 1), 1, 254)
    codes = (v * np.exp2(127.0 - byte)[:, None, :]).reshape(n, m).astype(np.float32).astype(ml_dtypes.float8_e4m3fn).view(np.uint8)
    words = codes.reshape(n // 512, 128, 4, m).transpose(0, 1, 3, 2)
    return np.ascontiguousarray(words), np.ascontiguousarray(byte.astype(np.uint8).reshape(n // 512, 16, m))


K, T, S, N, H, W = 512, 2048, 512, 512, 512, 2048


def setup_inputs():
    n = np.random.standard_normal
    s = mx_kscale(K)[:, None]
    u = mx_kscale(H)
    packed_xT = pack_weight(n((K, T)) * s)
    packed_w1 = pack_fp4(n((K, H)) / np.sqrt(K) / s)
    packed_w2 = pack_fp4(n((K, H)) / np.sqrt(K) / s)
    packed_w3 = pack_fp4(n((H, N)) / np.sqrt(2 * H) / u[:, None])
    packed_w4 = pack_fp4(n((H, N)) / np.sqrt(2 * H) / u[:, None])
    return {
        "x_words": packed_xT[0],
        "x_scales": packed_xT[1],
        "w1_words": packed_w1[0],
        "w1_scales": packed_w1[1],
        "w2_words": packed_w2[0],
        "w2_scales": packed_w2[1],
        "gn": (np.random.uniform(0.5, 1.5, (H, 1)) * u[:, None]).astype(np.float32),
        "gm": (np.random.uniform(0.5, 1.5, (H, 1)) * u[:, None]).astype(np.float32),
        "w3_words": packed_w3[0],
        "w3_scales": packed_w3[1],
        "w4_words": packed_w4[0],
        "w4_scales": packed_w4[1],
        "offs": striped(np.random.permutation(T)[:S]),
        "hz": striped8(np.random.randint(0, T, (8, S))),
        "n1": striped(np.random.permutation(S)),
        "n2": striped(np.random.permutation(S)),
        "n3": striped(np.random.permutation(S)),
        "n4": striped(np.random.permutation(S)),
        "n5": striped(np.random.permutation(S)),
        "n6": striped(np.random.randint(0, S, W)),
    }


def reference(x_words, x_scales, w1_words, w1_scales, w2_words, w2_scales, gn, gm, w3_words, w3_scales, w4_words, w4_scales, offs, hz, n1, n2, n3, n4, n5, n6):
    xq = unpack_weight(x_words, x_scales)[:, unstriped(offs)]
    y = unpack_fp4(w1_words, w1_scales).T @ xq
    rl = relu(y)
    ds = np.zeros((H, S))
    ds[:, unstriped(n1)] = rl
    z = f64(gn) * (ds - (0.5 * y))
    x_hz = unpack_weight(x_words, x_scales)[np.arange(K)[:, None], runs(hz, K)]
    d = unpack_fp4(w2_words, w2_scales).T @ x_hz
    z2 = f64(gm) * (0.75 * (d[:, unstriped(n2)] * d[:, unstriped(n3)] - (d[:, unstriped(n4)] * d[:, unstriped(n5)])))
    h = unpack_fp4(w3_words, w3_scales).T @ mxq(z, 0, "e4m3") + unpack_fp4(w4_words, w4_scales).T @ mxq(z2, 0, "e4m3")
    mb = h[:, unstriped(n6)]
    mx = mb.reshape(N, S, 4).max(axis=2)
    mn = mb.reshape(N, S, 4).min(axis=2)
    out_0 = np.maximum(np.minimum(1.5 * h, mx), mn)
    return (out_0,) + planes(out_0)

@@ -1,0 +1,279 @@
+from contextlib import ExitStack
+
+import concourse.mybir as mybir
+
+K, T, S, H, N, MEMBERS = 512, 2048, 512, 512, 512, 4
+FLOPS = 2 * (2 * K * H * S + 2 * H * N * S)
+
+F32 = mybir.dt.float32
+BF16 = mybir.dt.bfloat16
+I32 = mybir.dt.int32
+U32 = mybir.dt.uint32
+U16 = mybir.dt.uint16
+U8 = mybir.dt.uint8
+FP8X4 = mybir.dt.float8_e4m3fn_x4
+FP4X4 = mybir.dt.float4_e2m1fn_x4
+ALU = mybir.AluOpType
+COPY = mybir.ActivationFunctionType.Copy
+
+P = 128
+PACK = 4
+LIST_ROWS = 16
+CHUNK = 128
+SPARE = 16
+
+
+def entries(offsets, start, count):
+    return offsets[:, start // LIST_ROWS : (start + count) // LIST_ROWS]
+
+
+def by_word(tile):
+    return tile[:].rearrange("p (c i t) -> p c t i", i=4, t=PACK)
+
+
+def by_row(tile):
+    return tile[:].rearrange("p t (c i) -> p c t i", i=4)
+
+
+def tile_picked_hjoinsenddetgclip_none_po_kernel(
+    tc, x_words, x_scales, w1_words, w1_scales, w2_words, w2_scales, gn, gm,
+    w3_words, w3_scales, w4_words, w4_scales, offs, hz, n1, n2, n3, n4, n5, n6,
+    out_0, out_1, out_2,
+):
+    nc = tc.nc
+    with ExitStack() as ctx:
+        held = ctx.enter_context(tc.tile_pool(name="held", bufs=1))
+        psum = ctx.enter_context(tc.psum_pool(name="psum", bufs=4))
+
+        def load_list(source, name):
+            tile = held.tile(list(source.shape), U16, name=name)
+            nc.sync.dma_start(tile[:], source)
+            return tile
+
+        def load_weight_words(source, name, queue):
+            tile = held.tile([P, 2 * H], U8, name=name, tag=name)
+            queue.dma_start(tile[:].bitcast(I32), source[0].bitcast(I32))
+            return tile
+
+        def load_scale_rows(target, source):
+            nc.sync.dma_start(target[0:P:8, :].bitcast(I32), source[0].bitcast(I32))
+
+        def cleared(width, name, engine):
+            tile = held.tile([P, width], U8, name=name)
+            engine.memset(tile[:].bitcast(I32), 0)
+            return tile
+
+        def place_scale_rows(plane, source, queue):
+            for i in range(1, 4):
+                queue.dma_start(plane[i:P:32, :].bitcast(I32), source[8 * i : P : 32, :].bitcast(I32))
+
+        def deal_words(raw, name):
+            dealt = held.tile([P, 2 * H], U8, name=name, align_bytes=64)
+            nc.vector.tensor_copy(
+                out=dealt[:].rearrange("p (t m b) -> p t m b", t=PACK, b=2),
+                in_=raw[:].rearrange("p (m t b) -> p t m b", t=PACK, b=2),
+            )
+            return dealt
+
+        def deal_scales(raw, name, queue):
+            dealt = held.tile([P, 2 * H], U8, name=name, align_bytes=64)
+            nc.vector.tensor_copy(
+                out=dealt[:].rearrange("p (w t m) -> p w t m", w=2, t=PACK),
+                in_=raw[:].rearrange("p (w m t) -> p w t m", w=2, t=PACK),
+            )
+            place_scale_rows(dealt, dealt, queue)
+            return dealt[:, 0:H], dealt[:, H : 2 * H]
+
+        def pick_scales(offsets, name, queue):
+            picked = held.tile([P, S], U8, name=name + "_picked")
+            nc.vector.tensor_copy(picked[:], x_scale_rows[:].indirect(offsets[:]))
+            plane = held.tile([P, S], U8, name=name + "_plane", align_bytes=64)
+            nc.vector.tensor_copy(plane[:].bitcast(I32), picked[:].bitcast(I32))
+            place_scale_rows(plane, picked, queue)
+            return plane
+
+        def pick_words(offsets, name):
+            picked = held.tile([P, S], U32, name=name, align_bytes=64)
+            nc.vector.tensor_copy(picked[:], x_table[:].indirect(offsets[:]))
+            return picked
+
+        def mx_pass(out, w_words, w_plane, t, codes, plane, start, stop):
+            nc.tensor.matmul_mx(
+                out=out,
+                lhsT=w_words[:, 2 * P * t : 2 * P * (t + 1)].bitcast(FP4X4),
+                lhsT_scale=w_plane[:, P * t : P * (t + 1)],
+                rhs=codes.bitcast(FP8X4),
+                rhs_scale=plane,
+                start=start,
+                stop=stop,
+            )
+
+        def quantize(rounded, width, name):
+            codes = held.tile([P, width], U32, name=name + "_codes", align_bytes=64)
+            plane = held.tile([P, width], U8, name=name + "_plane", align_bytes=64)
+            nc.vector.quantize_mx(out=codes[:].bitcast(FP8X4), scales=plane[:], in_=rounded[:])
+            return codes, plane
+
+        x_scale_rows = cleared(T, "x_scale_rows", nc.gpsimd)
+        w_scale_rows = cleared(2 * H, "w_scale_rows", nc.vector)
+        hz_list = load_list(hz, "hz_list")
+        load_scale_rows(x_scale_rows, x_scales)
+        load_scale_rows(w_scale_rows[:, H : 2 * H], w2_scales)
+        load_scale_rows(w_scale_rows[:, 0:H], w1_scales)
+        w2_raw = load_weight_words(w2_words, "w_raw_b", nc.sync)
+        offs_list = load_list(offs, "offs_list")
+        w1_raw = load_weight_words(w1_words, "w_raw_a", nc.sync)
+        x_table = held.tile([P, T], U32, name="x_table")
+        nc.sync.dma_start(x_table[:].bitcast(I32), x_words[0].rearrange("p n t -> p (n t)").bitcast(I32))
+
+        hz_plane = pick_scales(hz_list, "hz_scales", nc.scalar)
+        w1_plane, w2_plane = deal_scales(w_scale_rows, "w12_planes", nc.scalar)
+        w2_dealt = deal_words(w2_raw, "w2_dealt")
+        hz_words = pick_words(hz_list, "hz_words")
+
+        gn_cols = held.tile([P, PACK], F32, name="gn_cols")
+        gm_cols = held.tile([P, PACK], F32, name="gm_cols")
+        nc.gpsimd.dma_start(gm_cols[:], gm.rearrange("(p t) o -> p (t o)", t=PACK))
+        nc.gpsimd.dma_start(gn_cols[:], gn.rearrange("(p t) o -> p (t o)", t=PACK))
+        n2_list, n4_list = load_list(n2, "n2_list"), load_list(n4, "n4_list")
+        n3_list, n5_list = load_list(n3, "n3_list"), load_list(n5, "n5_list")
+        n1_list = load_list(n1, "n1_list")
+        gm_scaled = held.tile([P, PACK], F32, name="gm_scaled")
+        gn_half = held.tile([P, PACK], F32, name="gn_half")
+        nc.scalar.activation(gm_scaled[:], gm_cols[:], COPY, scale=0.75)
+        nc.scalar.activation(gn_half[:], gn_cols[:], COPY, scale=-0.5)
+
+        d_rows, d_gained = [], []
+        for t in range(PACK):
+            bank = psum.tile([P, S], F32, name="d_bank", tag="d_then_h")
+            mx_pass(bank[:], w2_dealt, w2_plane, t, hz_words[:], hz_plane[:], True, True)
+            rows = held.tile([P, S], F32, name=f"d_rows{t}")
+            nc.scalar.activation(rows[:], bank[:], COPY)
+            d_rows.append(rows)
+
+        offs_plane = pick_scales(offs_list, "offs_scales", nc.sync)
+        offs_words = pick_words(offs_list, "offs_words")
+        w1_dealt = deal_words(w1_raw, "w1_dealt")
+        for t in range(PACK):
+            gained = held.tile([P, S], F32, name=f"d_gained{t}")
+            nc.vector.tensor_scalar(gained[:], d_rows[t][:], gm_scaled[:, t : t + 1], None, ALU.mult)
+            d_gained.append(gained)
+
+        y_banks, sent = [], []
+        for t in range(PACK):
+            bank = psum.tile([P, S], F32, name="y_bank", tag="y")
+            mx_pass(bank[:], w1_dealt, w1_plane, t, offs_words[:], offs_plane[:], True, True)
+            positive = held.tile([P, S], F32, name=f"positive{t}")
+            nc.vector.tensor_scalar(positive[:], bank[:], 0.0, gn_cols[:, t : t + 1], ALU.max, ALU.mult)
+            y_banks.append(bank)
+            sent.append(positive)
+
+        n6_list = load_list(n6, "n6_list")
+        load_scale_rows(w_scale_rows[:, 0:H], w3_scales)
+        load_scale_rows(w_scale_rows[:, H : 2 * H], w4_scales)
+        w3_raw = load_weight_words(w3_words, "w_raw_a", nc.sync)
+        w4_raw = load_weight_words(w4_words, "w_raw_b", nc.sync)
+
+        def fetch_first_factors(start, width, on_scalar):
+            firsts = []
+            for name, offsets in (("n2", n2_list), ("n4", n4_list)):
+                firsts.append(held.tile([P, PACK, width], F32, name=f"{name}_at{start}"))
+            for t in range(PACK):
+                for first, offsets in zip(firsts, (n2_list, n4_list)):
+                    window = d_gained[t][:].indirect(entries(offsets, start, width))
+                    if on_scalar:
+                        nc.scalar.activation(first[:, t, :], window, COPY)
+                    else:
+                        nc.vector.tensor_copy(first[:, t, :], window)
+            return firsts
+
+        def finish_z2(firsts, start, width):
+            products = [held.tile([P, PACK, width], F32, name=f"product{s}_at{start}") for s in range(2)]
+            for t in range(PACK):
+                for product, first, offsets in zip(products, firsts, (n3_list, n5_list)):
+                    window = d_rows[t][:].indirect(entries(offsets, start, width))
+                    nc.vector.tensor_tensor(product[:, t, :], window, first[:, t, :], ALU.mult)
+            rounded = held.tile([P, PACK * width], BF16, name=f"z2_rounded{start}", align_bytes=64)
+            nc.vector.tensor_tensor(by_word(rounded), by_row(products[0]), by_row(products[1]), ALU.subtract)
+            codes, plane = quantize(rounded, width, f"z2_at{start}")
+            return [(codes[:, c : c + CHUNK], plane[:, c : c + CHUNK]) for c in range(0, width, CHUNK)]
+
+        z2_chunks = []
+        firsts0 = fetch_first_factors(0, 256, True)
+        placed = []
+        for t in range(PACK):
+            window = held.tile([P, S], F32, name=f"placed{t}")
+            for start in range(0, S, S // 2):
+                nc.scalar.activation(
+                    window[:].indirect(entries(n1_list, start, S // 2)), sent[t][:, start : start + S // 2], COPY
+                )
+            placed.append(window)
+        z2_chunks.extend(finish_z2(firsts0, 0, 256))
+        w3_plane, w4_plane = deal_scales(w_scale_rows, "w34_planes", nc.sync)
+        w3_dealt = deal_words(w3_raw, "w3_dealt")
+        w4_dealt = deal_words(w4_raw, "w4_dealt")
+        z2_chunks.extend(finish_z2(fetch_first_factors(256, 128, False), 256, 128))
+
+        z_rows = held.tile([P, PACK, S], F32, name="z_rows")
+        for t in range(PACK):
+            nc.vector.scalar_tensor_tensor(
+                z_rows[:, t, :], y_banks[t][:], gn_half[:, t : t + 1], placed[t][:], ALU.mult, ALU.add
+            )
+        z_rounded = held.tile([P, PACK * S], BF16, name="z_rounded", align_bytes=64)
+        nc.vector.tensor_copy(by_word(z_rounded), by_row(z_rows))
+        z_codes, z_plane = quantize(z_rounded, S, "z")
+        z2_chunks.extend(finish_z2(fetch_first_factors(384, 128, True), 384, 128))
+
+        h_rows = [held.tile([P, S + SPARE], F32, name=f"h_rows{t}") for t in range(PACK)]
+        for rows in h_rows:
+            nc.gpsimd.memset(rows[:, S:], 0.0)
+        h_banks = []
+        for c in range(S // CHUNK):
+            cols = slice(c * CHUNK, (c + 1) * CHUNK)
+            bank = psum.tile([P, PACK, CHUNK], F32, name="h_bank", tag="d_then_h")
+            for t in range(PACK):
+                mx_pass(bank[:, t, :], w3_dealt, w3_plane, t, z_codes[:, cols], z_plane[:, cols], t == 0, False)
+            for t in range(PACK):
+                mx_pass(bank[:, t, :], w4_dealt, w4_plane, t, *z2_chunks[c], False, t == PACK - 1)
+            for t in range(PACK):
+                nc.scalar.activation(h_rows[t][:, cols], bank[:, t, :], COPY)
+            h_banks.append(bank)
+
+        out_codes = held.tile([P, S], U32, name="out_codes", align_bytes=64)
+        out_plane = held.tile([P, S], U8, name="out_plane", align_bytes=64)
+        out_rows = out_0.rearrange("(p t) j -> p t j", t=PACK)
+        out_words = out_1[0].rearrange("p j t -> p (j t)").bitcast(I32)
+        for c in range(S // CHUNK):
+            cols = slice(c * CHUNK, (c + 1) * CHUNK)
+            result = held.tile([P, PACK, CHUNK], F32, name=f"result{c}")
+            step = 1 if c in (0, S // CHUNK - 1) else 2
+            for t0 in range(0, PACK, step):
+                name = f"{c}_{t0}"
+                members = held.tile([P, step * CHUNK, MEMBERS], F32, name="members" + name)
+                flat = members[:].rearrange("p j m -> p (j m)")
+                for t in range(t0, t0 + step):
+                    window = h_rows[t][:].indirect(entries(n6_list, c * CHUNK * MEMBERS, CHUNK * MEMBERS))
+                    at = (t - t0) * CHUNK * MEMBERS
+                    nc.scalar.activation(flat[:, at : at + CHUNK * MEMBERS], window, COPY)
+                pair_max = held.tile([P, step * CHUNK, 2], F32, name="pair_max" + name)
+                pair_min = held.tile([P, step * CHUNK, 2], F32, name="pair_min" + name)
+                largest = held.tile([P, step * CHUNK], F32, name="largest" + name)
+                smallest = held.tile([P, step * CHUNK], F32, name="smallest" + name)
+                capped = held.tile([P, step * CHUNK], F32, name="capped" + name)
+                nc.vector.tensor_tensor(pair_max[:], members[:, :, 0:2], members[:, :, 2:4], ALU.max)
+                nc.vector.tensor_tensor(pair_min[:], members[:, :, 0:2], members[:, :, 2:4], ALU.min)
+                nc.vector.tensor_tensor(largest[:], pair_max[:, :, 0], pair_max[:, :, 1], ALU.max)
+                nc.vector.tensor_tensor(smallest[:], pair_min[:, :, 0], pair_min[:, :, 1], ALU.min)
+                h_here = h_banks[c][:, t0 : t0 + step, :].rearrange("p t j -> p (t j)")
+                nc.vector.scalar_tensor_tensor(capped[:], h_here, 1.5, largest[:], ALU.mult, ALU.min)
+                nc.vector.tensor_tensor(
+                    result[:, t0 : t0 + step, :].rearrange("p t j -> p (t j)"), capped[:], smallest[:], ALU.max
+                )
+            nc.sync.dma_start(out_rows[:, :, cols], result[:])
+            rounded = held.tile([P, PACK * CHUNK], BF16, name=f"out_rounded{c}", align_bytes=64)
+            nc.vector.tensor_copy(by_word(rounded), by_row(result))
+            nc.vector.quantize_mx(out=out_codes[:, cols].bitcast(FP8X4), scales=out_plane[:, cols], in_=rounded[:])
+            nc.sync.dma_start(out_words[:, cols], out_codes[:, cols].bitcast(I32))
+        for i in range(4):
+            queue = nc.sync if i % 2 else nc.scalar
+            queue.dma_start(out_2[0, i:16:4, :].bitcast(I32), out_plane[i:P:32, :].bitcast(I32))

@@ -43,6 +43,7 @@ def tile_picked_hjoinsenddetgclip_none_po_kernel(
     nc = tc.nc
     with ExitStack() as ctx:
         held = ctx.enter_context(tc.tile_pool(name="held", bufs=1))
+        ring = ctx.enter_context(tc.tile_pool(name="ring", bufs=2))
         psum = ctx.enter_context(tc.psum_pool(name="psum", bufs=4))
 
         def load_list(source, name):
@@ -70,8 +71,8 @@ def tile_picked_hjoinsenddetgclip_none_po_kernel(
         def deal_words(raw, name):
             dealt = held.tile([P, 2 * H], U8, name=name, align_bytes=64)
             nc.vector.tensor_copy(
-                out=dealt[:].rearrange("p (t m b) -> p t m b", t=PACK, b=2),
-                in_=raw[:].rearrange("p (m t b) -> p t m b", t=PACK, b=2),
+                out=dealt[:].bitcast(U16).rearrange("p (t m) -> p t m", t=PACK),
+                in_=raw[:].bitcast(U16).rearrange("p (m t) -> p t m", t=PACK),
             )
             return dealt
 
@@ -194,7 +195,9 @@ def tile_picked_hjoinsenddetgclip_none_po_kernel(
                     window = d_rows[t][:].indirect(entries(offsets, start, width))
                     nc.vector.tensor_tensor(product[:, t, :], window, first[:, t, :], ALU.mult)
             rounded = held.tile([P, PACK * width], BF16, name=f"z2_rounded{start}", align_bytes=64)
-            nc.vector.tensor_tensor(by_word(rounded), by_row(products[0]), by_row(products[1]), ALU.subtract)
+            difference = held.tile([P, PACK, width], F32, name=f"difference{start}")
+            nc.vector.tensor_tensor(difference[:], products[0][:], products[1][:], ALU.subtract)
+            nc.vector.tensor_copy(by_word(rounded), by_row(difference))
             codes, plane = quantize(rounded, width, f"z2_at{start}")
             return [(codes[:, c : c + CHUNK], plane[:, c : c + CHUNK]) for c in range(0, width, CHUNK)]
 
@@ -243,37 +246,57 @@ def tile_picked_hjoinsenddetgclip_none_po_kernel(
         out_plane = held.tile([P, S], U8, name="out_plane", align_bytes=64)
         out_rows = out_0.rearrange("(p t) j -> p t j", t=PACK)
         out_words = out_1[0].rearrange("p j t -> p (j t)").bitcast(I32)
-        for c in range(S // CHUNK):
-            cols = slice(c * CHUNK, (c + 1) * CHUNK)
-            result = held.tile([P, PACK, CHUNK], F32, name=f"result{c}")
-            step = 1 if c in (0, S // CHUNK - 1) else 2
-            for t0 in range(0, PACK, step):
-                name = f"{c}_{t0}"
-                members = held.tile([P, step * CHUNK, MEMBERS], F32, name="members" + name)
-                flat = members[:].rearrange("p j m -> p (j m)")
-                for t in range(t0, t0 + step):
-                    window = h_rows[t][:].indirect(entries(n6_list, c * CHUNK * MEMBERS, CHUNK * MEMBERS))
-                    at = (t - t0) * CHUNK * MEMBERS
+        chunks = S // CHUNK
+        step = 2
+
+        def clip_group(c, t0, result):
+            members = ring.tile([P, step * CHUNK, MEMBERS], F32, name="members")
+            flat = members[:].rearrange("p j m -> p (j m)")
+            for t in range(t0, t0 + step):
+                window = h_rows[t][:].indirect(entries(n6_list, c * CHUNK * MEMBERS, CHUNK * MEMBERS))
+                at = (t - t0) * CHUNK * MEMBERS
+                if c == 0 and t == 1:
+                    nc.vector.tensor_copy(flat[:, at : at + CHUNK * MEMBERS], window)
+                else:
                     nc.scalar.activation(flat[:, at : at + CHUNK * MEMBERS], window, COPY)
-                pair_max = held.tile([P, step * CHUNK, 2], F32, name="pair_max" + name)
-                pair_min = held.tile([P, step * CHUNK, 2], F32, name="pair_min" + name)
-                largest = held.tile([P, step * CHUNK], F32, name="largest" + name)
-                smallest = held.tile([P, step * CHUNK], F32, name="smallest" + name)
-                capped = held.tile([P, step * CHUNK], F32, name="capped" + name)
-                nc.vector.tensor_tensor(pair_max[:], members[:, :, 0:2], members[:, :, 2:4], ALU.max)
-                nc.vector.tensor_tensor(pair_min[:], members[:, :, 0:2], members[:, :, 2:4], ALU.min)
-                nc.vector.tensor_tensor(largest[:], pair_max[:, :, 0], pair_max[:, :, 1], ALU.max)
-                nc.vector.tensor_tensor(smallest[:], pair_min[:, :, 0], pair_min[:, :, 1], ALU.min)
-                h_here = h_banks[c][:, t0 : t0 + step, :].rearrange("p t j -> p (t j)")
-                nc.vector.scalar_tensor_tensor(capped[:], h_here, 1.5, largest[:], ALU.mult, ALU.min)
-                nc.vector.tensor_tensor(
-                    result[:, t0 : t0 + step, :].rearrange("p t j -> p (t j)"), capped[:], smallest[:], ALU.max
-                )
-            nc.sync.dma_start(out_rows[:, :, cols], result[:])
+            pair_max = ring.tile([P, step * CHUNK, 2], F32, name="pair_max")
+            pair_min = ring.tile([P, step * CHUNK, 2], F32, name="pair_min")
+            largest = ring.tile([P, step * CHUNK], F32, name="largest")
+            smallest = ring.tile([P, step * CHUNK], F32, name="smallest")
+            capped = ring.tile([P, step * CHUNK], F32, name="capped")
+            nc.vector.tensor_tensor(pair_max[:], members[:, :, 0:2], members[:, :, 2:4], ALU.max)
+            nc.vector.tensor_tensor(pair_min[:], members[:, :, 0:2], members[:, :, 2:4], ALU.min)
+            nc.vector.tensor_tensor(largest[:], pair_max[:, :, 0], pair_max[:, :, 1], ALU.max)
+            nc.vector.tensor_tensor(smallest[:], pair_min[:, :, 0], pair_min[:, :, 1], ALU.min)
+            h_here = h_banks[c][:, t0 : t0 + step, :].rearrange("p t j -> p (t j)")
+            nc.vector.scalar_tensor_tensor(capped[:], h_here, 1.5, largest[:], ALU.mult, ALU.min)
+            nc.vector.tensor_tensor(
+                result[:, t0 : t0 + step, :].rearrange("p t j -> p (t j)"), capped[:], smallest[:], ALU.max
+            )
+
+        def round_result(c, result):
+            nc.sync.dma_start(out_rows[:, :, c * CHUNK : (c + 1) * CHUNK], result[:])
             rounded = held.tile([P, PACK * CHUNK], BF16, name=f"out_rounded{c}", align_bytes=64)
-            nc.vector.tensor_copy(by_word(rounded), by_row(result))
+            if c < chunks - 1:
+                nc.scalar.copy(by_word(rounded), by_row(result))
+            else:
+                nc.vector.tensor_copy(by_word(rounded), by_row(result))
+            return rounded
+
+        def quantize_result(c, rounded):
+            cols = slice(c * CHUNK, (c + 1) * CHUNK)
             nc.vector.quantize_mx(out=out_codes[:, cols].bitcast(FP8X4), scales=out_plane[:, cols], in_=rounded[:])
             nc.sync.dma_start(out_words[:, cols], out_codes[:, cols].bitcast(I32))
+
+        waiting = None
+        for c in range(chunks):
+            result = held.tile([P, PACK, CHUNK], F32, name=f"result{c}")
+            for t0 in range(0, PACK, step):
+                clip_group(c, t0, result)
+            if waiting is not None:
+                quantize_result(c - 1, waiting)
+            waiting = round_result(c, result)
+        quantize_result(chunks - 1, waiting)
         for i in range(4):
             queue = nc.sync if i % 2 else nc.scalar
             queue.dma_start(out_2[0, i:16:4, :].bitcast(I32), out_plane[i:P:32, :].bitcast(I32))

@@ -15,11 +15,12 @@ FP8X4 = mybir.dt.float8_e4m3fn_x4
 FP4X4 = mybir.dt.float4_e2m1fn_x4
 ALU = mybir.AluOpType
 COPY = mybir.ActivationFunctionType.Copy
+RELU = mybir.ActivationFunctionType.Relu
 
 P = 128
 PACK = 4
 LIST_ROWS = 16
-CHUNK = 128
+HALF = S // 2
 SPARE = 16
 
 
@@ -52,15 +53,19 @@ def tile_picked_hjoinsenddetgclip_none_po_kernel(
             return tile
 
         def load_weight_words(source, name, queue):
-            tile = held.tile([P, 2 * H], U8, name=name, tag=name)
+            tile = held.tile([P, 2 * H], U8, name=name, tag=name, align_bytes=64)
             queue.dma_start(tile[:].bitcast(I32), source[0].bitcast(I32))
             return tile
 
-        def load_scale_rows(target, source):
+        def load_scale_rows(target, source, queue):
+            for i in range(4):
+                queue.dma_start(target[i:P:32, :].bitcast(I32), source[0, i:16:4, :].bitcast(I32))
+
+        def load_scale_rows_spread(target, source):
             nc.sync.dma_start(target[0:P:8, :].bitcast(I32), source[0].bitcast(I32))
 
         def cleared(width, name, engine):
-            tile = held.tile([P, width], U8, name=name)
+            tile = held.tile([P, width], U8, name=name, tag=name, align_bytes=64)
             engine.memset(tile[:].bitcast(I32), 0)
             return tile
 
@@ -76,25 +81,21 @@ def tile_picked_hjoinsenddetgclip_none_po_kernel(
             )
             return dealt
 
-        def deal_scales(raw, name, queue):
-            dealt = held.tile([P, 2 * H], U8, name=name, align_bytes=64)
+        def deal_scales(raw, name):
+            dealt = held.tile([P, H], U8, name=name, tag=name, align_bytes=64)
             nc.vector.tensor_copy(
-                out=dealt[:].rearrange("p (w t m) -> p w t m", w=2, t=PACK),
-                in_=raw[:].rearrange("p (w m t) -> p w t m", w=2, t=PACK),
+                out=dealt[:].rearrange("p (t m) -> p t m", t=PACK),
+                in_=raw[:].rearrange("p (m t) -> p t m", t=PACK),
             )
-            place_scale_rows(dealt, dealt, queue)
-            return dealt[:, 0:H], dealt[:, H : 2 * H]
+            return dealt
 
-        def pick_scales(offsets, name, queue):
-            picked = held.tile([P, S], U8, name=name + "_picked")
-            nc.vector.tensor_copy(picked[:], x_scale_rows[:].indirect(offsets[:]))
-            plane = held.tile([P, S], U8, name=name + "_plane", align_bytes=64)
-            nc.vector.tensor_copy(plane[:].bitcast(I32), picked[:].bitcast(I32))
-            place_scale_rows(plane, picked, queue)
-            return plane
+        def pick_scales(rows, offsets, name):
+            picked = held.tile([P, S], U8, name=name, tag=name, align_bytes=64)
+            nc.vector.tensor_copy(picked[:], rows[:].indirect(offsets[:]))
+            return picked
 
         def pick_words(offsets, name):
-            picked = held.tile([P, S], U32, name=name, align_bytes=64)
+            picked = held.tile([P, S], U32, name=name, tag="picked_words_then_staged", align_bytes=64)
             nc.vector.tensor_copy(picked[:], x_table[:].indirect(offsets[:]))
             return picked
 
@@ -115,188 +116,195 @@ def tile_picked_hjoinsenddetgclip_none_po_kernel(
             nc.vector.quantize_mx(out=codes[:].bitcast(FP8X4), scales=plane[:], in_=rounded[:])
             return codes, plane
 
-        x_scale_rows = cleared(T, "x_scale_rows", nc.gpsimd)
-        w_scale_rows = cleared(2 * H, "w_scale_rows", nc.vector)
-        hz_list = load_list(hz, "hz_list")
-        load_scale_rows(x_scale_rows, x_scales)
-        load_scale_rows(w_scale_rows[:, H : 2 * H], w2_scales)
-        load_scale_rows(w_scale_rows[:, 0:H], w1_scales)
-        w2_raw = load_weight_words(w2_words, "w_raw_b", nc.sync)
-        offs_list = load_list(offs, "offs_list")
-        w1_raw = load_weight_words(w1_words, "w_raw_a", nc.sync)
+        x_rows_placed = cleared(T, "x_rows_placed", nc.gpsimd)
+        x_rows_spread = cleared(T, "x_rows_spread", nc.vector)
+        w1_rows = cleared(H, "w1_rows_then_hz_picked", nc.gpsimd)
+        w2_rows = cleared(H, "w2_rows", nc.gpsimd)
         x_table = held.tile([P, T], U32, name="x_table")
-        nc.sync.dma_start(x_table[:].bitcast(I32), x_words[0].rearrange("p n t -> p (n t)").bitcast(I32))
-
-        hz_plane = pick_scales(hz_list, "hz_scales", nc.scalar)
-        w1_plane, w2_plane = deal_scales(w_scale_rows, "w12_planes", nc.scalar)
-        w2_dealt = deal_words(w2_raw, "w2_dealt")
-        hz_words = pick_words(hz_list, "hz_words")
+        x_source = x_words[0].rearrange("p n t -> p (n t)").bitcast(I32)
+        nc.sync.dma_start(x_table[:, : T // 2].bitcast(I32), x_source[:, : T // 2])
+        load_scale_rows(x_rows_placed, x_scales, nc.sync)
+        offs_list = load_list(offs, "offs_list")
+        w1_raw = load_weight_words(w1_words, "w1_raw", nc.sync)
+        nc.sync.dma_start(x_table[:, T // 2 :].bitcast(I32), x_source[:, T // 2 :])
+        load_scale_rows(w1_rows, w1_scales, nc.sync)
+        hz_list = load_list(hz, "hz_list")
+        load_scale_rows_spread(x_rows_spread, x_scales)
+        n1_list = load_list(n1, "n1_list")
+        w2_raw = load_weight_words(w2_words, "w2_raw", nc.sync)
 
         gn_cols = held.tile([P, PACK], F32, name="gn_cols")
         gm_cols = held.tile([P, PACK], F32, name="gm_cols")
-        nc.gpsimd.dma_start(gm_cols[:], gm.rearrange("(p t) o -> p (t o)", t=PACK))
         nc.gpsimd.dma_start(gn_cols[:], gn.rearrange("(p t) o -> p (t o)", t=PACK))
+        load_scale_rows(w2_rows, w2_scales, nc.gpsimd)
+        nc.gpsimd.dma_start(gm_cols[:], gm.rearrange("(p t) o -> p (t o)", t=PACK))
+        gn_half = held.tile([P, PACK], F32, name="gn_half")
+        nc.scalar.activation(gn_half[:], gn_cols[:], COPY, scale=-0.5)
+
+        offs_plane = pick_scales(x_rows_placed, offs_list, "offs_then_w2_plane")
+        w1_dealt = deal_words(w1_raw, "w1_dealt")
+        offs_words = pick_words(offs_list, "offs_words")
+        w1_plane = deal_scales(w1_rows, "w1_plane")
+        y_banks = []
+        for t in range(PACK):
+            bank = psum.tile([P, S], F32, name="y_bank", tag="y")
+            mx_pass(bank[:], w1_dealt, w1_plane, t, offs_words[:], offs_plane[:], True, True)
+            y_banks.append(bank)
+
+        def send(positive, tag):
+            window = held.tile([P, S], F32, name="placed", tag=tag)
+            for start in range(0, S, HALF):
+                nc.scalar.activation(
+                    window[:].indirect(entries(n1_list, start, HALF)), positive[:, start : start + HALF], COPY
+                )
+            return window
+
+        positives = [held.tile([P, S], F32, name=f"positive{t}") for t in range(PACK)]
+        ungained = held.tile([P, S], F32, name="ungained")
+        nc.scalar.activation(ungained[:], y_banks[0][:], RELU)
+        nc.scalar.activation(positives[0][:], ungained[:], COPY, scale=gn_cols[:, 0:1])
+        placed = [send(positives[0], "placed0")]
+
+        hz_picked = pick_scales(x_rows_spread, hz_list, "w1_rows_then_hz_picked")
+        hz_plane = held.tile([P, S], U8, name="hz_plane", tag="hz_plane_then_w_rows", align_bytes=64)
+        nc.vector.tensor_copy(hz_plane[:].bitcast(I32), hz_picked[:].bitcast(I32))
+        place_scale_rows(hz_plane, hz_picked, nc.sync)
+        hz_words = pick_words(hz_list, "hz_words")
+        w2_dealt = deal_words(w2_raw, "w2_dealt")
+        w2_plane = deal_scales(w2_rows, "offs_then_w2_plane")
         n2_list, n4_list = load_list(n2, "n2_list"), load_list(n4, "n4_list")
         n3_list, n5_list = load_list(n3, "n3_list"), load_list(n5, "n5_list")
-        n1_list = load_list(n1, "n1_list")
-        gm_scaled = held.tile([P, PACK], F32, name="gm_scaled")
-        gn_half = held.tile([P, PACK], F32, name="gn_half")
-        nc.scalar.activation(gm_scaled[:], gm_cols[:], COPY, scale=0.75)
-        nc.scalar.activation(gn_half[:], gn_cols[:], COPY, scale=-0.5)
 
         d_rows, d_gained = [], []
         for t in range(PACK):
             bank = psum.tile([P, S], F32, name="d_bank", tag="d_then_h")
             mx_pass(bank[:], w2_dealt, w2_plane, t, hz_words[:], hz_plane[:], True, True)
-            rows = held.tile([P, S], F32, name=f"d_rows{t}")
-            nc.scalar.activation(rows[:], bank[:], COPY)
+            rows = held.tile([P, S + SPARE], F32, name=f"d_rows{t}")
+            nc.gpsimd.memset(rows[:, S:], 0.0)
+            nc.scalar.activation(rows[:, :S], bank[:], COPY)
+            gained = held.tile([P, S + SPARE], F32, name="d_gained", tag=f"gained_then_placed{t}")
+            nc.vector.tensor_scalar(gained[:], rows[:], gm_cols[:, t : t + 1], 0.75, ALU.mult, ALU.mult)
             d_rows.append(rows)
-
-        offs_plane = pick_scales(offs_list, "offs_scales", nc.sync)
-        offs_words = pick_words(offs_list, "offs_words")
-        w1_dealt = deal_words(w1_raw, "w1_dealt")
-        for t in range(PACK):
-            gained = held.tile([P, S], F32, name=f"d_gained{t}")
-            nc.vector.tensor_scalar(gained[:], d_rows[t][:], gm_scaled[:, t : t + 1], None, ALU.mult)
             d_gained.append(gained)
-
-        y_banks, sent = [], []
-        for t in range(PACK):
-            bank = psum.tile([P, S], F32, name="y_bank", tag="y")
-            mx_pass(bank[:], w1_dealt, w1_plane, t, offs_words[:], offs_plane[:], True, True)
-            positive = held.tile([P, S], F32, name=f"positive{t}")
-            nc.vector.tensor_scalar(positive[:], bank[:], 0.0, gn_cols[:, t : t + 1], ALU.max, ALU.mult)
-            y_banks.append(bank)
-            sent.append(positive)
+        for t in range(1, PACK):
+            nc.vector.tensor_scalar(positives[t][:], y_banks[t][:], 0.0, gn_cols[:, t : t + 1], ALU.max, ALU.mult)
 
         n6_list = load_list(n6, "n6_list")
-        load_scale_rows(w_scale_rows[:, 0:H], w3_scales)
-        load_scale_rows(w_scale_rows[:, H : 2 * H], w4_scales)
-        w3_raw = load_weight_words(w3_words, "w_raw_a", nc.sync)
-        w4_raw = load_weight_words(w4_words, "w_raw_b", nc.sync)
+        w_rows = cleared(H, "hz_plane_then_w_rows", nc.gpsimd)
+        load_scale_rows(w_rows, w4_scales, nc.sync)
+        w4_dealt = deal_words(load_weight_words(w4_words, "picked_words_then_staged", nc.sync), "w4_dealt")
+        w4_plane = deal_scales(w_rows, "w4_plane")
+        load_scale_rows(w_rows, w3_scales, nc.sync)
+        w3_dealt = deal_words(load_weight_words(w3_words, "picked_words_then_staged", nc.sync), "w3_dealt")
+        w3_plane = deal_scales(w_rows, "w3_plane")
 
-        def fetch_first_factors(start, width, on_scalar):
-            firsts = []
-            for name, offsets in (("n2", n2_list), ("n4", n4_list)):
-                firsts.append(held.tile([P, PACK, width], F32, name=f"{name}_at{start}"))
-            for t in range(PACK):
-                for first, offsets in zip(firsts, (n2_list, n4_list)):
-                    window = d_gained[t][:].indirect(entries(offsets, start, width))
-                    if on_scalar:
-                        nc.scalar.activation(first[:, t, :], window, COPY)
-                    else:
-                        nc.vector.tensor_copy(first[:, t, :], window)
-            return firsts
-
-        def finish_z2(firsts, start, width):
-            products = [held.tile([P, PACK, width], F32, name=f"product{s}_at{start}") for s in range(2)]
-            for t in range(PACK):
-                for product, first, offsets in zip(products, firsts, (n3_list, n5_list)):
-                    window = d_rows[t][:].indirect(entries(offsets, start, width))
-                    nc.vector.tensor_tensor(product[:, t, :], window, first[:, t, :], ALU.mult)
-            rounded = held.tile([P, PACK * width], BF16, name=f"z2_rounded{start}", align_bytes=64)
-            difference = held.tile([P, PACK, width], F32, name=f"difference{start}")
-            nc.vector.tensor_tensor(difference[:], products[0][:], products[1][:], ALU.subtract)
-            nc.vector.tensor_copy(by_word(rounded), by_row(difference))
-            codes, plane = quantize(rounded, width, f"z2_at{start}")
-            return [(codes[:, c : c + CHUNK], plane[:, c : c + CHUNK]) for c in range(0, width, CHUNK)]
-
-        z2_chunks = []
-        firsts0 = fetch_first_factors(0, 256, True)
-        placed = []
+        firsts = [held.tile([P, PACK, S], F32, name=f"first{s}") for s in range(2)]
+        products = [held.tile([P, PACK, S], F32, name=f"product{s}") for s in range(2)]
         for t in range(PACK):
-            window = held.tile([P, S], F32, name=f"placed{t}")
-            for start in range(0, S, S // 2):
-                nc.scalar.activation(
-                    window[:].indirect(entries(n1_list, start, S // 2)), sent[t][:, start : start + S // 2], COPY
-                )
-            placed.append(window)
-        z2_chunks.extend(finish_z2(firsts0, 0, 256))
-        w3_plane, w4_plane = deal_scales(w_scale_rows, "w34_planes", nc.sync)
-        w3_dealt = deal_words(w3_raw, "w3_dealt")
-        w4_dealt = deal_words(w4_raw, "w4_dealt")
-        z2_chunks.extend(finish_z2(fetch_first_factors(256, 128, False), 256, 128))
+            for first, offsets in zip(firsts, (n2_list, n4_list)):
+                if t > 0:
+                    nc.scalar.activation(first[:, t, :], d_gained[t][:].indirect(offsets[:]), COPY)
+                else:
+                    for start in range(0, S, HALF):
+                        window = d_gained[t][:].indirect(entries(offsets, start, HALF))
+                        nc.vector.tensor_copy(first[:, t, start : start + HALF], window)
+            for product, first, offsets in zip(products, firsts, (n3_list, n5_list)):
+                nc.vector.tensor_tensor(product[:, t, :], d_rows[t][:].indirect(offsets[:]), first[:, t, :], ALU.mult)
+        for t in range(1, PACK):
+            placed.append(send(positives[t], f"gained_then_placed{PACK - t}"))
+        z2_rounded = held.tile([P, PACK * S], BF16, name="z2_rounded", align_bytes=64)
+        nc.vector.tensor_tensor(by_word(z2_rounded), by_row(products[0]), by_row(products[1]), ALU.subtract)
+        z2_codes, z2_plane = quantize(z2_rounded, S, "z2")
+        h_banks = []
+        for t in range(PACK):
+            bank = psum.tile([P, S], F32, name="h_bank", tag="d_then_h")
+            mx_pass(bank[:], w4_dealt, w4_plane, t, z2_codes[:], z2_plane[:], True, False)
+            h_banks.append(bank)
 
         z_rows = held.tile([P, PACK, S], F32, name="z_rows")
         for t in range(PACK):
             nc.vector.scalar_tensor_tensor(
                 z_rows[:, t, :], y_banks[t][:], gn_half[:, t : t + 1], placed[t][:], ALU.mult, ALU.add
             )
-        z_rounded = held.tile([P, PACK * S], BF16, name="z_rounded", align_bytes=64)
-        nc.vector.tensor_copy(by_word(z_rounded), by_row(z_rows))
-        z_codes, z_plane = quantize(z_rounded, S, "z")
-        z2_chunks.extend(finish_z2(fetch_first_factors(384, 128, True), 384, 128))
+        z_rounded = [held.tile([P, PACK * HALF], BF16, name=f"z_rounded{c}", align_bytes=64) for c in range(2)]
+        nc.vector.tensor_copy(by_word(z_rounded[0]), by_row(z_rows[:, :, :HALF]))
+        nc.scalar.copy(by_word(z_rounded[1]), by_row(z_rows[:, :, HALF:]))
+        for c in range(2):
+            cols = slice(c * HALF, (c + 1) * HALF)
+            z_codes, z_plane = quantize(z_rounded[c], HALF, f"z{c}")
+            for t in range(PACK):
+                mx_pass(h_banks[t][:, cols], w3_dealt, w3_plane, t, z_codes[:], z_plane[:], False, c == 1)
 
         h_rows = [held.tile([P, S + SPARE], F32, name=f"h_rows{t}") for t in range(PACK)]
         for rows in h_rows:
             nc.gpsimd.memset(rows[:, S:], 0.0)
-        h_banks = []
-        for c in range(S // CHUNK):
-            cols = slice(c * CHUNK, (c + 1) * CHUNK)
-            bank = psum.tile([P, PACK, CHUNK], F32, name="h_bank", tag="d_then_h")
-            for t in range(PACK):
-                mx_pass(bank[:, t, :], w3_dealt, w3_plane, t, z_codes[:, cols], z_plane[:, cols], t == 0, False)
-            for t in range(PACK):
-                mx_pass(bank[:, t, :], w4_dealt, w4_plane, t, *z2_chunks[c], False, t == PACK - 1)
-            for t in range(PACK):
-                nc.scalar.activation(h_rows[t][:, cols], bank[:, t, :], COPY)
-            h_banks.append(bank)
-
         out_codes = held.tile([P, S], U32, name="out_codes", align_bytes=64)
         out_plane = held.tile([P, S], U8, name="out_plane", align_bytes=64)
         out_rows = out_0.rearrange("(p t) j -> p t j", t=PACK)
         out_words = out_1[0].rearrange("p j t -> p (j t)").bitcast(I32)
-        chunks = S // CHUNK
-        step = 2
+        results = [held.tile([P, PACK, HALF], F32, name=f"result{c}") for c in range(2)]
+        out_rounded = [held.tile([P, PACK * HALF], BF16, name=f"out_rounded{c}", align_bytes=64) for c in range(2)]
 
-        def clip_group(c, t0, result):
-            members = ring.tile([P, step * CHUNK, MEMBERS], F32, name="members")
-            flat = members[:].rearrange("p j m -> p (j m)")
-            for t in range(t0, t0 + step):
-                window = h_rows[t][:].indirect(entries(n6_list, c * CHUNK * MEMBERS, CHUNK * MEMBERS))
-                at = (t - t0) * CHUNK * MEMBERS
-                if c == 0 and t == 1:
-                    nc.vector.tensor_copy(flat[:, at : at + CHUNK * MEMBERS], window)
-                else:
-                    nc.scalar.activation(flat[:, at : at + CHUNK * MEMBERS], window, COPY)
-            pair_max = ring.tile([P, step * CHUNK, 2], F32, name="pair_max")
-            pair_min = ring.tile([P, step * CHUNK, 2], F32, name="pair_min")
-            largest = ring.tile([P, step * CHUNK], F32, name="largest")
-            smallest = ring.tile([P, step * CHUNK], F32, name="smallest")
-            capped = ring.tile([P, step * CHUNK], F32, name="capped")
-            nc.vector.tensor_tensor(pair_max[:], members[:, :, 0:2], members[:, :, 2:4], ALU.max)
-            nc.vector.tensor_tensor(pair_min[:], members[:, :, 0:2], members[:, :, 2:4], ALU.min)
-            nc.vector.tensor_tensor(largest[:], pair_max[:, :, 0], pair_max[:, :, 1], ALU.max)
-            nc.vector.tensor_tensor(smallest[:], pair_min[:, :, 0], pair_min[:, :, 1], ALU.min)
-            h_here = h_banks[c][:, t0 : t0 + step, :].rearrange("p t j -> p (t j)")
-            nc.vector.scalar_tensor_tensor(capped[:], h_here, 1.5, largest[:], ALU.mult, ALU.min)
-            nc.vector.tensor_tensor(
-                result[:, t0 : t0 + step, :].rearrange("p t j -> p (t j)"), capped[:], smallest[:], ALU.max
-            )
-
-        def round_result(c, result):
-            nc.sync.dma_start(out_rows[:, :, c * CHUNK : (c + 1) * CHUNK], result[:])
-            rounded = held.tile([P, PACK * CHUNK], BF16, name=f"out_rounded{c}", align_bytes=64)
-            if c < chunks - 1:
-                nc.scalar.copy(by_word(rounded), by_row(result))
+        def empty_h(t):
+            if t == 1:
+                nc.vector.tensor_copy(h_rows[t][:, :S], h_banks[t][:])
             else:
-                nc.vector.tensor_copy(by_word(rounded), by_row(result))
-            return rounded
+                nc.scalar.activation(h_rows[t][:, :S], h_banks[t][:], COPY)
 
-        def quantize_result(c, rounded):
-            cols = slice(c * CHUNK, (c + 1) * CHUNK)
-            nc.vector.quantize_mx(out=out_codes[:, cols].bitcast(FP8X4), scales=out_plane[:, cols], in_=rounded[:])
+        def fetch_members(c, t):
+            members = ring.tile([P, HALF, MEMBERS], F32, name="members")
+            flat = members[:].rearrange("p j m -> p (j m)")
+            for at in range(0, HALF * MEMBERS, S):
+                window = h_rows[t][:].indirect(entries(n6_list, c * HALF * MEMBERS + at, S))
+                if (c, t, at) == (0, 0, S):
+                    nc.vector.tensor_copy(flat[:, at : at + S], window)
+                else:
+                    nc.scalar.activation(flat[:, at : at + S], window, COPY)
+            return members
+
+        def raise_and_store(c, t, capped, smallest):
+            nc.vector.tensor_tensor(results[c][:, t, :], capped[:], smallest[:], ALU.max)
+            nc.sync.dma_start(out_rows[:, t, c * HALF : (c + 1) * HALF], results[c][:, t, :])
+
+        def quantize_result(c):
+            cols = slice(c * HALF, (c + 1) * HALF)
+            nc.vector.quantize_mx(out=out_codes[:, cols].bitcast(FP8X4), scales=out_plane[:, cols], in_=out_rounded[c][:])
             nc.sync.dma_start(out_words[:, cols], out_codes[:, cols].bitcast(I32))
 
-        waiting = None
-        for c in range(chunks):
-            result = held.tile([P, PACK, CHUNK], F32, name=f"result{c}")
-            for t0 in range(0, PACK, step):
-                clip_group(c, t0, result)
-            if waiting is not None:
-                quantize_result(c - 1, waiting)
-            waiting = round_result(c, result)
-        quantize_result(chunks - 1, waiting)
+        empty_h(0)
+        empty_h(1)
+        unfinished = None
+        for c in range(2):
+            for t in range(PACK):
+                if c == 0 and t >= 2:
+                    empty_h(t)
+                members = fetch_members(c, t)
+                pair_max = ring.tile([P, HALF, 2], F32, name="pair_max")
+                pair_min = ring.tile([P, HALF, 2], F32, name="pair_min")
+                largest = ring.tile([P, HALF], F32, name="largest")
+                smallest = ring.tile([P, HALF], F32, name="smallest")
+                capped = ring.tile([P, HALF], F32, name="capped")
+                width = HALF // 2 if (c, t) == (1, PACK - 1) else HALF
+                for at in range(0, HALF, width):
+                    part = slice(at, at + width)
+                    low, high = members[:, part, 0:2], members[:, part, 2:4]
+                    nc.vector.tensor_tensor(pair_max[:, part, :], low, high, ALU.max)
+                    if unfinished is not None:
+                        raise_and_store(*unfinished)
+                        unfinished = None
+                    nc.vector.tensor_tensor(pair_min[:, part, :], low, high, ALU.min)
+                nc.vector.tensor_tensor(largest[:], pair_max[:, :, 0], pair_max[:, :, 1], ALU.max)
+                nc.vector.tensor_tensor(smallest[:], pair_min[:, :, 0], pair_min[:, :, 1], ALU.min)
+                h_here = h_banks[t][:, c * HALF : (c + 1) * HALF]
+                nc.vector.scalar_tensor_tensor(capped[:], h_here, 1.5, largest[:], ALU.mult, ALU.min)
+                unfinished = (c, t, capped, smallest)
+                if (c, t) == (1, 0):
+                    nc.scalar.copy(by_word(out_rounded[0]), by_row(results[0]))
+                if (c, t) == (1, 2):
+                    quantize_result(0)
+        raise_and_store(*unfinished)
+        nc.vector.tensor_copy(by_word(out_rounded[1]), by_row(results[1]))
+        quantize_result(1)
         for i in range(4):
             queue = nc.sync if i % 2 else nc.scalar
             queue.dma_start(out_2[0, i:16:4, :].bitcast(I32), out_plane[i:P:32, :].bitcast(I32))

@@ -70,11 +70,11 @@ def tile_picked_hjoinsenddetgclip_none_po_kernel(
             return tile
 
         def place_scale_rows(plane, source, queue):
-            for i in range(1, 4):
+            for i in range(4):
                 queue.dma_start(plane[i:P:32, :].bitcast(I32), source[8 * i : P : 32, :].bitcast(I32))
 
         def deal_words(raw, name):
-            dealt = held.tile([P, 2 * H], U8, name=name, align_bytes=64)
+            dealt = held.tile([P, 2 * H], U8, name=name, tag=name, align_bytes=64)
             nc.vector.tensor_copy(
                 out=dealt[:].bitcast(U16).rearrange("p (t m) -> p t m", t=PACK),
                 in_=raw[:].bitcast(U16).rearrange("p (m t) -> p t m", t=PACK),
@@ -95,7 +95,7 @@ def tile_picked_hjoinsenddetgclip_none_po_kernel(
             return picked
 
         def pick_words(offsets, name):
-            picked = held.tile([P, S], U32, name=name, tag="picked_words_then_staged", align_bytes=64)
+            picked = held.tile([P, S], U32, name=name, tag=name, align_bytes=64)
             nc.vector.tensor_copy(picked[:], x_table[:].indirect(offsets[:]))
             return picked
 
@@ -117,31 +117,32 @@ def tile_picked_hjoinsenddetgclip_none_po_kernel(
             return codes, plane
 
         x_rows_placed = cleared(T, "x_rows_placed", nc.gpsimd)
-        x_rows_spread = cleared(T, "x_rows_spread", nc.vector)
+        x_rows_spread = cleared(T, "spread_rows_then_hz_words", nc.vector)
         w1_rows = cleared(H, "w1_rows_then_hz_picked", nc.gpsimd)
-        w2_rows = cleared(H, "w2_rows", nc.gpsimd)
-        x_table = held.tile([P, T], U32, name="x_table")
+        w_rows = cleared(H, "w_rows", nc.gpsimd)
+        hz_plane = cleared(S, "hz_plane", nc.vector)
+        x_table = held.tile([P, T], U32, name="x_table", tag="x_table_then_positives")
         x_source = x_words[0].rearrange("p n t -> p (n t)").bitcast(I32)
         nc.sync.dma_start(x_table[:, : T // 2].bitcast(I32), x_source[:, : T // 2])
         load_scale_rows(x_rows_placed, x_scales, nc.sync)
         offs_list = load_list(offs, "offs_list")
-        w1_raw = load_weight_words(w1_words, "w1_raw", nc.sync)
+        w1_raw = load_weight_words(w1_words, "w1_then_w3_raw", nc.sync)
         nc.sync.dma_start(x_table[:, T // 2 :].bitcast(I32), x_source[:, T // 2 :])
         load_scale_rows(w1_rows, w1_scales, nc.sync)
         hz_list = load_list(hz, "hz_list")
         load_scale_rows_spread(x_rows_spread, x_scales)
         n1_list = load_list(n1, "n1_list")
-        w2_raw = load_weight_words(w2_words, "w2_raw", nc.sync)
+        w2_raw = load_weight_words(w2_words, "w2_then_w4_raw", nc.sync)
 
         gn_cols = held.tile([P, PACK], F32, name="gn_cols")
         gm_cols = held.tile([P, PACK], F32, name="gm_cols")
         nc.gpsimd.dma_start(gn_cols[:], gn.rearrange("(p t) o -> p (t o)", t=PACK))
-        load_scale_rows(w2_rows, w2_scales, nc.gpsimd)
+        load_scale_rows(w_rows, w2_scales, nc.gpsimd)
         nc.gpsimd.dma_start(gm_cols[:], gm.rearrange("(p t) o -> p (t o)", t=PACK))
         gn_half = held.tile([P, PACK], F32, name="gn_half")
         nc.scalar.activation(gn_half[:], gn_cols[:], COPY, scale=-0.5)
 
-        offs_plane = pick_scales(x_rows_placed, offs_list, "offs_then_w2_plane")
+        offs_plane = pick_scales(x_rows_placed, offs_list, "offs_plane")
         w1_dealt = deal_words(w1_raw, "w1_dealt")
         offs_words = pick_words(offs_list, "offs_words")
         w1_plane = deal_scales(w1_rows, "w1_plane")
@@ -159,19 +160,17 @@ def tile_picked_hjoinsenddetgclip_none_po_kernel(
                 )
             return window
 
-        positives = [held.tile([P, S], F32, name=f"positive{t}") for t in range(PACK)]
+        first_positive = held.tile([P, S], F32, name="first_positive")
         ungained = held.tile([P, S], F32, name="ungained")
         nc.scalar.activation(ungained[:], y_banks[0][:], RELU)
-        nc.scalar.activation(positives[0][:], ungained[:], COPY, scale=gn_cols[:, 0:1])
-        placed = [send(positives[0], "placed0")]
+        nc.scalar.activation(first_positive[:], ungained[:], COPY, scale=gn_cols[:, 0:1])
+        placed = [send(first_positive, "placed0")]
 
         hz_picked = pick_scales(x_rows_spread, hz_list, "w1_rows_then_hz_picked")
-        hz_plane = held.tile([P, S], U8, name="hz_plane", tag="hz_plane_then_w_rows", align_bytes=64)
-        nc.vector.tensor_copy(hz_plane[:].bitcast(I32), hz_picked[:].bitcast(I32))
         place_scale_rows(hz_plane, hz_picked, nc.sync)
-        hz_words = pick_words(hz_list, "hz_words")
-        w2_dealt = deal_words(w2_raw, "w2_dealt")
-        w2_plane = deal_scales(w2_rows, "offs_then_w2_plane")
+        hz_words = pick_words(hz_list, "spread_rows_then_hz_words")
+        w2_dealt = deal_words(w2_raw, "w2_dealt_then_z_rows")
+        w2_plane = deal_scales(w_rows, "w1_rows_then_hz_picked")
         n2_list, n4_list = load_list(n2, "n2_list"), load_list(n4, "n4_list")
         n3_list, n5_list = load_list(n3, "n3_list"), load_list(n5, "n5_list")
 
@@ -180,22 +179,22 @@ def tile_picked_hjoinsenddetgclip_none_po_kernel(
             bank = psum.tile([P, S], F32, name="d_bank", tag="d_then_h")
             mx_pass(bank[:], w2_dealt, w2_plane, t, hz_words[:], hz_plane[:], True, True)
             rows = held.tile([P, S + SPARE], F32, name=f"d_rows{t}")
-            nc.gpsimd.memset(rows[:, S:], 0.0)
+            nc.vector.memset(rows[:, S:], 0.0)
             nc.scalar.activation(rows[:, :S], bank[:], COPY)
             gained = held.tile([P, S + SPARE], F32, name="d_gained", tag=f"gained_then_placed{t}")
             nc.vector.tensor_scalar(gained[:], rows[:], gm_cols[:, t : t + 1], 0.75, ALU.mult, ALU.mult)
             d_rows.append(rows)
             d_gained.append(gained)
+        positives = held.tile([P, PACK - 1, S], F32, name="positives", tag="x_table_then_positives")
         for t in range(1, PACK):
-            nc.vector.tensor_scalar(positives[t][:], y_banks[t][:], 0.0, gn_cols[:, t : t + 1], ALU.max, ALU.mult)
+            nc.vector.tensor_scalar(positives[:, t - 1, :], y_banks[t][:], 0.0, gn_cols[:, t : t + 1], ALU.max, ALU.mult)
 
         n6_list = load_list(n6, "n6_list")
-        w_rows = cleared(H, "hz_plane_then_w_rows", nc.gpsimd)
         load_scale_rows(w_rows, w4_scales, nc.sync)
-        w4_dealt = deal_words(load_weight_words(w4_words, "picked_words_then_staged", nc.sync), "w4_dealt")
+        w4_dealt = deal_words(load_weight_words(w4_words, "w2_then_w4_raw", nc.sync), "w4_dealt")
         w4_plane = deal_scales(w_rows, "w4_plane")
         load_scale_rows(w_rows, w3_scales, nc.sync)
-        w3_dealt = deal_words(load_weight_words(w3_words, "picked_words_then_staged", nc.sync), "w3_dealt")
+        w3_dealt = deal_words(load_weight_words(w3_words, "w1_then_w3_raw", nc.sync), "w3_dealt")
         w3_plane = deal_scales(w_rows, "w3_plane")
 
         firsts = [held.tile([P, PACK, S], F32, name=f"first{s}") for s in range(2)]
@@ -211,7 +210,7 @@ def tile_picked_hjoinsenddetgclip_none_po_kernel(
             for product, first, offsets in zip(products, firsts, (n3_list, n5_list)):
                 nc.vector.tensor_tensor(product[:, t, :], d_rows[t][:].indirect(offsets[:]), first[:, t, :], ALU.mult)
         for t in range(1, PACK):
-            placed.append(send(positives[t], f"gained_then_placed{PACK - t}"))
+            placed.append(send(positives[:, t - 1, :], f"gained_then_placed{PACK - t}"))
         z2_rounded = held.tile([P, PACK * S], BF16, name="z2_rounded", align_bytes=64)
         nc.vector.tensor_tensor(by_word(z2_rounded), by_row(products[0]), by_row(products[1]), ALU.subtract)
         z2_codes, z2_plane = quantize(z2_rounded, S, "z2")
@@ -221,7 +220,7 @@ def tile_picked_hjoinsenddetgclip_none_po_kernel(
             mx_pass(bank[:], w4_dealt, w4_plane, t, z2_codes[:], z2_plane[:], True, False)
             h_banks.append(bank)
 
-        z_rows = held.tile([P, PACK, S], F32, name="z_rows")
+        z_rows = held.tile([P, PACK, S], F32, name="z_rows", tag="w2_dealt_then_z_rows", align_bytes=64)
         for t in range(PACK):
             nc.vector.scalar_tensor_tensor(
                 z_rows[:, t, :], y_banks[t][:], gn_half[:, t : t + 1], placed[t][:], ALU.mult, ALU.add
@@ -237,7 +236,7 @@ def tile_picked_hjoinsenddetgclip_none_po_kernel(
 
         h_rows = [held.tile([P, S + SPARE], F32, name=f"h_rows{t}") for t in range(PACK)]
         for rows in h_rows:
-            nc.gpsimd.memset(rows[:, S:], 0.0)
+            nc.vector.memset(rows[:, S:], 0.0)
         out_codes = held.tile([P, S], U32, name="out_codes", align_bytes=64)
         out_plane = held.tile([P, S], U8, name="out_plane", align_bytes=64)
         out_rows = out_0.rearrange("(p t) j -> p t j", t=PACK)

from contextlib import ExitStack

import concourse.mybir as mybir

K, T, S, H, N, MEMBERS = 512, 2048, 512, 512, 512, 4
FLOPS = 2 * (2 * K * H * S + 2 * H * N * S)

F32 = mybir.dt.float32
BF16 = mybir.dt.bfloat16
I32 = mybir.dt.int32
U32 = mybir.dt.uint32
U16 = mybir.dt.uint16
U8 = mybir.dt.uint8
FP8X4 = mybir.dt.float8_e4m3fn_x4
FP4X4 = mybir.dt.float4_e2m1fn_x4
ALU = mybir.AluOpType
COPY = mybir.ActivationFunctionType.Copy
RELU = mybir.ActivationFunctionType.Relu

P = 128
PACK = 4
LIST_ROWS = 16
HALF = S // 2
SPARE = 16


def entries(offsets, start, count):
    return offsets[:, start // LIST_ROWS : (start + count) // LIST_ROWS]


def by_word(tile):
    return tile[:].rearrange("p (c i t) -> p c t i", i=4, t=PACK)


def by_row(tile):
    return tile[:].rearrange("p t (c i) -> p c t i", i=4)


def tile_picked_hjoinsenddetgclip_none_po_kernel(
    tc, x_words, x_scales, w1_words, w1_scales, w2_words, w2_scales, gn, gm,
    w3_words, w3_scales, w4_words, w4_scales, offs, hz, n1, n2, n3, n4, n5, n6,
    out_0, out_1, out_2,
):
    nc = tc.nc
    with ExitStack() as ctx:
        held = ctx.enter_context(tc.tile_pool(name="held", bufs=1))
        ring = ctx.enter_context(tc.tile_pool(name="ring", bufs=2))
        psum = ctx.enter_context(tc.psum_pool(name="psum", bufs=4))

        def load_list(source, name):
            tile = held.tile(list(source.shape), U16, name=name)
            nc.sync.dma_start(tile[:], source)
            return tile

        def load_weight_words(source, name, queue):
            tile = held.tile([P, 2 * H], U8, name=name, tag=name, align_bytes=64)
            queue.dma_start(tile[:].bitcast(I32), source[0].bitcast(I32))
            return tile

        def load_scale_rows(target, source, queue):
            for i in range(4):
                queue.dma_start(target[i:P:32, :].bitcast(I32), source[0, i:16:4, :].bitcast(I32))

        def load_scale_rows_spread(target, source):
            nc.sync.dma_start(target[0:P:8, :].bitcast(I32), source[0].bitcast(I32))

        def cleared(width, name, engine):
            tile = held.tile([P, width], U8, name=name, tag=name, align_bytes=64)
            engine.memset(tile[:].bitcast(I32), 0)
            return tile

        def place_scale_rows(plane, source, queue):
            for i in range(4):
                queue.dma_start(plane[i:P:32, :].bitcast(I32), source[8 * i : P : 32, :].bitcast(I32))

        def deal_words(raw, name):
            dealt = held.tile([P, 2 * H], U8, name=name, tag=name, align_bytes=64)
            nc.vector.tensor_copy(
                out=dealt[:].bitcast(U16).rearrange("p (t m) -> p t m", t=PACK),
                in_=raw[:].bitcast(U16).rearrange("p (m t) -> p t m", t=PACK),
            )
            return dealt

        def deal_scales(raw, name):
            dealt = held.tile([P, H], U8, name=name, tag=name, align_bytes=64)
            nc.vector.tensor_copy(
                out=dealt[:].rearrange("p (t m) -> p t m", t=PACK),
                in_=raw[:].rearrange("p (m t) -> p t m", t=PACK),
            )
            return dealt

        def pick_scales(rows, offsets, name):
            picked = held.tile([P, S], U8, name=name, tag=name, align_bytes=64)
            nc.vector.tensor_copy(picked[:], rows[:].indirect(offsets[:]))
            return picked

        def pick_words(offsets, name):
            picked = held.tile([P, S], U32, name=name, tag=name, align_bytes=64)
            nc.vector.tensor_copy(picked[:], x_table[:].indirect(offsets[:]))
            return picked

        def mx_pass(out, w_words, w_plane, t, codes, plane, start, stop):
            nc.tensor.matmul_mx(
                out=out,
                lhsT=w_words[:, 2 * P * t : 2 * P * (t + 1)].bitcast(FP4X4),
                lhsT_scale=w_plane[:, P * t : P * (t + 1)],
                rhs=codes.bitcast(FP8X4),
                rhs_scale=plane,
                start=start,
                stop=stop,
            )

        def quantize(rounded, width, name):
            codes = held.tile([P, width], U32, name=name + "_codes", align_bytes=64)
            plane = held.tile([P, width], U8, name=name + "_plane", align_bytes=64)
            nc.vector.quantize_mx(out=codes[:].bitcast(FP8X4), scales=plane[:], in_=rounded[:])
            return codes, plane

        x_rows_placed = cleared(T, "x_rows_placed", nc.gpsimd)
        x_rows_spread = cleared(T, "spread_rows_then_hz_words", nc.vector)
        w1_rows = cleared(H, "w1_rows_then_hz_picked", nc.gpsimd)
        w_rows = cleared(H, "w_rows", nc.gpsimd)
        hz_plane = cleared(S, "hz_plane", nc.vector)
        x_table = held.tile([P, T], U32, name="x_table", tag="x_table_then_positives")
        x_source = x_words[0].rearrange("p n t -> p (n t)").bitcast(I32)
        nc.sync.dma_start(x_table[:, : T // 2].bitcast(I32), x_source[:, : T // 2])
        load_scale_rows(x_rows_placed, x_scales, nc.sync)
        offs_list = load_list(offs, "offs_list")
        w1_raw = load_weight_words(w1_words, "w1_then_w3_raw", nc.sync)
        nc.sync.dma_start(x_table[:, T // 2 :].bitcast(I32), x_source[:, T // 2 :])
        load_scale_rows(w1_rows, w1_scales, nc.sync)
        hz_list = load_list(hz, "hz_list")
        load_scale_rows_spread(x_rows_spread, x_scales)
        n1_list = load_list(n1, "n1_list")
        w2_raw = load_weight_words(w2_words, "w2_then_w4_raw", nc.sync)

        gn_cols = held.tile([P, PACK], F32, name="gn_cols")
        gm_cols = held.tile([P, PACK], F32, name="gm_cols")
        nc.gpsimd.dma_start(gn_cols[:], gn.rearrange("(p t) o -> p (t o)", t=PACK))
        load_scale_rows(w_rows, w2_scales, nc.gpsimd)
        nc.gpsimd.dma_start(gm_cols[:], gm.rearrange("(p t) o -> p (t o)", t=PACK))
        gn_half = held.tile([P, PACK], F32, name="gn_half")
        nc.scalar.activation(gn_half[:], gn_cols[:], COPY, scale=-0.5)

        offs_plane = pick_scales(x_rows_placed, offs_list, "offs_plane")
        w1_dealt = deal_words(w1_raw, "w1_dealt")
        offs_words = pick_words(offs_list, "offs_words")
        w1_plane = deal_scales(w1_rows, "w1_plane")
        y_banks = []
        for t in range(PACK):
            bank = psum.tile([P, S], F32, name="y_bank", tag="y")
            mx_pass(bank[:], w1_dealt, w1_plane, t, offs_words[:], offs_plane[:], True, True)
            y_banks.append(bank)

        def send(positive, tag):
            window = held.tile([P, S], F32, name="placed", tag=tag)
            for start in range(0, S, HALF):
                nc.scalar.activation(
                    window[:].indirect(entries(n1_list, start, HALF)), positive[:, start : start + HALF], COPY
                )
            return window

        first_positive = held.tile([P, S], F32, name="first_positive")
        ungained = held.tile([P, S], F32, name="ungained")
        nc.scalar.activation(ungained[:], y_banks[0][:], RELU)
        nc.scalar.activation(first_positive[:], ungained[:], COPY, scale=gn_cols[:, 0:1])
        placed = [send(first_positive, "placed0")]

        hz_picked = pick_scales(x_rows_spread, hz_list, "w1_rows_then_hz_picked")
        place_scale_rows(hz_plane, hz_picked, nc.sync)
        hz_words = pick_words(hz_list, "spread_rows_then_hz_words")
        w2_dealt = deal_words(w2_raw, "w2_dealt_then_z_rows")
        w2_plane = deal_scales(w_rows, "w1_rows_then_hz_picked")
        n2_list, n4_list = load_list(n2, "n2_list"), load_list(n4, "n4_list")
        n3_list, n5_list = load_list(n3, "n3_list"), load_list(n5, "n5_list")

        d_rows, d_gained = [], []
        for t in range(PACK):
            bank = psum.tile([P, S], F32, name="d_bank", tag="d_then_h")
            mx_pass(bank[:], w2_dealt, w2_plane, t, hz_words[:], hz_plane[:], True, True)
            rows = held.tile([P, S + SPARE], F32, name=f"d_rows{t}")
            nc.vector.memset(rows[:, S:], 0.0)
            nc.scalar.activation(rows[:, :S], bank[:], COPY)
            gained = held.tile([P, S + SPARE], F32, name="d_gained", tag=f"gained_then_placed{t}")
            nc.vector.tensor_scalar(gained[:], rows[:], gm_cols[:, t : t + 1], 0.75, ALU.mult, ALU.mult)
            d_rows.append(rows)
            d_gained.append(gained)
        positives = held.tile([P, PACK - 1, S], F32, name="positives", tag="x_table_then_positives")
        for t in range(1, PACK):
            nc.vector.tensor_scalar(positives[:, t - 1, :], y_banks[t][:], 0.0, gn_cols[:, t : t + 1], ALU.max, ALU.mult)

        n6_list = load_list(n6, "n6_list")
        load_scale_rows(w_rows, w4_scales, nc.sync)
        w4_dealt = deal_words(load_weight_words(w4_words, "w2_then_w4_raw", nc.sync), "w4_dealt")
        w4_plane = deal_scales(w_rows, "w4_plane")
        load_scale_rows(w_rows, w3_scales, nc.sync)
        w3_dealt = deal_words(load_weight_words(w3_words, "w1_then_w3_raw", nc.sync), "w3_dealt")
        w3_plane = deal_scales(w_rows, "w3_plane")

        firsts = [held.tile([P, PACK, S], F32, name=f"first{s}") for s in range(2)]
        products = [held.tile([P, PACK, S], F32, name=f"product{s}") for s in range(2)]
        for t in range(PACK):
            for first, offsets in zip(firsts, (n2_list, n4_list)):
                if t > 0:
                    nc.scalar.activation(first[:, t, :], d_gained[t][:].indirect(offsets[:]), COPY)
                else:
                    for start in range(0, S, HALF):
                        window = d_gained[t][:].indirect(entries(offsets, start, HALF))
                        nc.vector.tensor_copy(first[:, t, start : start + HALF], window)
            for product, first, offsets in zip(products, firsts, (n3_list, n5_list)):
                nc.vector.tensor_tensor(product[:, t, :], d_rows[t][:].indirect(offsets[:]), first[:, t, :], ALU.mult)
        for t in range(1, PACK):
            placed.append(send(positives[:, t - 1, :], f"gained_then_placed{PACK - t}"))
        z2_rounded = held.tile([P, PACK * S], BF16, name="z2_rounded", align_bytes=64)
        nc.vector.tensor_tensor(by_word(z2_rounded), by_row(products[0]), by_row(products[1]), ALU.subtract)
        z2_codes, z2_plane = quantize(z2_rounded, S, "z2")
        h_banks = []
        for t in range(PACK):
            bank = psum.tile([P, S], F32, name="h_bank", tag="d_then_h")
            mx_pass(bank[:], w4_dealt, w4_plane, t, z2_codes[:], z2_plane[:], True, False)
            h_banks.append(bank)

        z_rows = held.tile([P, PACK, S], F32, name="z_rows", tag="w2_dealt_then_z_rows", align_bytes=64)
        for t in range(PACK):
            nc.vector.scalar_tensor_tensor(
                z_rows[:, t, :], y_banks[t][:], gn_half[:, t : t + 1], placed[t][:], ALU.mult, ALU.add
            )
        z_rounded = [held.tile([P, PACK * HALF], BF16, name=f"z_rounded{c}", align_bytes=64) for c in range(2)]
        nc.vector.tensor_copy(by_word(z_rounded[0]), by_row(z_rows[:, :, :HALF]))
        nc.scalar.copy(by_word(z_rounded[1]), by_row(z_rows[:, :, HALF:]))
        for c in range(2):
            cols = slice(c * HALF, (c + 1) * HALF)
            z_codes, z_plane = quantize(z_rounded[c], HALF, f"z{c}")
            for t in range(PACK):
                mx_pass(h_banks[t][:, cols], w3_dealt, w3_plane, t, z_codes[:], z_plane[:], False, c == 1)

        h_rows = [held.tile([P, S + SPARE], F32, name=f"h_rows{t}") for t in range(PACK)]
        for rows in h_rows:
            nc.vector.memset(rows[:, S:], 0.0)
        out_codes = held.tile([P, S], U32, name="out_codes", align_bytes=64)
        out_plane = held.tile([P, S], U8, name="out_plane", align_bytes=64)
        out_rows = out_0.rearrange("(p t) j -> p t j", t=PACK)
        out_words = out_1[0].rearrange("p j t -> p (j t)").bitcast(I32)
        results = [held.tile([P, PACK, HALF], F32, name=f"result{c}") for c in range(2)]
        out_rounded = [held.tile([P, PACK * HALF], BF16, name=f"out_rounded{c}", align_bytes=64) for c in range(2)]

        def empty_h(t):
            if t == 1:
                nc.vector.tensor_copy(h_rows[t][:, :S], h_banks[t][:])
            else:
                nc.scalar.activation(h_rows[t][:, :S], h_banks[t][:], COPY)

        def fetch_members(c, t):
            members = ring.tile([P, HALF, MEMBERS], F32, name="members")
            flat = members[:].rearrange("p j m -> p (j m)")
            for at in range(0, HALF * MEMBERS, S):
                window = h_rows[t][:].indirect(entries(n6_list, c * HALF * MEMBERS + at, S))
                if (c, t, at) == (0, 0, S):
                    nc.vector.tensor_copy(flat[:, at : at + S], window)
                else:
                    nc.scalar.activation(flat[:, at : at + S], window, COPY)
            return members

        def raise_and_store(c, t, capped, smallest):
            nc.vector.tensor_tensor(results[c][:, t, :], capped[:], smallest[:], ALU.max)
            nc.sync.dma_start(out_rows[:, t, c * HALF : (c + 1) * HALF], results[c][:, t, :])

        def quantize_result(c):
            cols = slice(c * HALF, (c + 1) * HALF)
            nc.vector.quantize_mx(out=out_codes[:, cols].bitcast(FP8X4), scales=out_plane[:, cols], in_=out_rounded[c][:])
            nc.sync.dma_start(out_words[:, cols], out_codes[:, cols].bitcast(I32))

        empty_h(0)
        empty_h(1)
        unfinished = None
        for c in range(2):
            for t in range(PACK):
                if c == 0 and t >= 2:
                    empty_h(t)
                members = fetch_members(c, t)
                pair_max = ring.tile([P, HALF, 2], F32, name="pair_max")
                pair_min = ring.tile([P, HALF, 2], F32, name="pair_min")
                largest = ring.tile([P, HALF], F32, name="largest")
                smallest = ring.tile([P, HALF], F32, name="smallest")
                capped = ring.tile([P, HALF], F32, name="capped")
                width = HALF // 2 if (c, t) == (1, PACK - 1) else HALF
                for at in range(0, HALF, width):
                    part = slice(at, at + width)
                    low, high = members[:, part, 0:2], members[:, part, 2:4]
                    nc.vector.tensor_tensor(pair_max[:, part, :], low, high, ALU.max)
                    if unfinished is not None:
                        raise_and_store(*unfinished)
                        unfinished = None
                    nc.vector.tensor_tensor(pair_min[:, part, :], low, high, ALU.min)
                nc.vector.tensor_tensor(largest[:], pair_max[:, :, 0], pair_max[:, :, 1], ALU.max)
                nc.vector.tensor_tensor(smallest[:], pair_min[:, :, 0], pair_min[:, :, 1], ALU.min)
                h_here = h_banks[t][:, c * HALF : (c + 1) * HALF]
                nc.vector.scalar_tensor_tensor(capped[:], h_here, 1.5, largest[:], ALU.mult, ALU.min)
                unfinished = (c, t, capped, smallest)
                if (c, t) == (1, 0):
                    nc.scalar.copy(by_word(out_rounded[0]), by_row(results[0]))
                if (c, t) == (1, 2):
                    quantize_result(0)
        raise_and_store(*unfinished)
        nc.vector.tensor_copy(by_word(out_rounded[1]), by_row(results[1]))
        quantize_result(1)
        for i in range(4):
            queue = nc.sync if i % 2 else nc.scalar
            queue.dma_start(out_2[0, i:16:4, :].bitcast(I32), out_plane[i:P:32, :].bitcast(I32))
